import numpy as np
import ml_dtypes


def mxq(x, axis, fmt="e4m3"):
    dtype, down = {"e4m3": (ml_dtypes.float8_e4m3fn, 7), "e5m2": (ml_dtypes.float8_e5m2, 14)}[fmt]
    v = np.moveaxis(np.asarray(x, np.float32).astype(ml_dtypes.bfloat16).astype(np.float64), axis, -1)
    blocks = v.reshape(v.shape[:-1] + (-1, 32))
    amax = np.abs(blocks).max(-1, keepdims=True)
    byte = np.maximum(np.where(amax > 0, np.frexp(amax)[1] - 1 + 127, 0) - down, 1)
    scale = np.exp2(byte - 127.0)
    codes = (blocks / scale).astype(np.float32).astype(dtype).astype(np.float64)
    return np.moveaxis((codes * scale).reshape(v.shape), -1, axis)


WIDE = False


def mx_kscale(k):
    if not WIDE:
        return np.ones(k)
    levels = np.array([10, -10, 5, -5, 0])
    if k % 512:
        return np.exp2(np.random.permutation(np.resize(levels, k // 32))).repeat(32)
    a = np.empty((k // 512, 16))
    for p in range(k // 512):
        a[p, :8] = np.random.permutation(np.resize(levels, 8))
        for g in range(8):
            far = levels[np.abs(levels - a[p, g]) >= 10]
            a[p, g + 8] = far[np.random.randint(len(far))]
    return np.exp2(a.ravel()).repeat(32)


def f64(x):
    return np.asarray(x).astype(np.float64)


def striped(idx):
    return np.tile(idx.reshape(-1, 16).T, (8, 1)).astype(np.uint16)


def unstriped(offs):
    return offs[:16].T.reshape(-1).astype(np.int64)


E2M1 = np.array([0.0, 0.5, 1.0, 1.5, 2.0, 3.0, 4.0, 6.0, -0.0, -0.5, -1.0, -1.5, -2.0, -3.0, -4.0, -6.0])


def pack_weight(w, fmt):
    k, n = w.shape
    w = f64(np.asarray(w, np.float32).astype(ml_dtypes.bfloat16)).reshape(k // 32, 32, n)
    amax = np.abs(w).max(1)
    if fmt == "e4m3":
        byte = np.frexp(amax)[1] - 1 + 127 - 7
    else:
        mant, ex = np.frexp(amax / 6.0)
        byte = np.where(mant > 0.5, ex, ex - 1) + 127
    byte = np.clip(np.where(amax > 0, byte, 1), 1, 254)
    scaled = (w * np.exp2(127.0 - byte)[:, None, :]).reshape(k, n).astype(np.float32)
    by_word = np.ascontiguousarray(scaled.reshape(k // 512, 128, 4, n).transpose(0, 1, 3, 2))
    if fmt == "e4m3":
        words = by_word.astype(ml_dtypes.float8_e4m3fn).view(np.uint8)
    else:
        c = by_word.astype(ml_dtypes.float4_e2m1fn).view(np.uint8) & 0xF
        words = (c[..., 0::2] | (c[..., 1::2] << 4)).reshape(k // 512, 128, 2 * n)
    return np.ascontiguousarray(words), np.ascontiguousarray(byte.astype(np.uint8).reshape(k // 512, 16, n))


def unpack_weight(words, scales, fmt):
    g, _, n = scales.shape
    words = np.ascontiguousarray(words).reshape(g, 128, n, -1)
    if fmt == "e4m3":
        vals = words.view(ml_dtypes.float8_e4m3fn).astype(np.float64)
    else:
        nib = np.empty((g, 128, n, 4), np.uint8)
        nib[..., 0::2] = words & 0xF
        nib[..., 1::2] = words >> 4
        vals = E2M1[nib]
    vals = vals * np.repeat(np.exp2(scales.astype(np.float64) - 127.0), 8, axis=1)[..., None]
    return vals.transpose(0, 1, 3, 2).reshape(g * 512, n)


def gelu(v):
    return 0.5 * v * (1.0 + np.tanh(np.sqrt(2.0 / np.pi) * (v + 0.044715 * v**3)))


K, H, N, T, S, P = 1024, 1024, 512, 4096, 1024, 512

def setup_inputs():
    n = np.random.standard_normal
    s = mx_kscale(K)[:, None]
    u = mx_kscale(H)[:, None]
    tab_words, tab_scales = pack_weight(n((K, T)) * s, "e4m3")
    wr_words, wr_scales = pack_weight(n((H, N)) / np.sqrt(H) / u, "e2m1")
    return {
        "tab_words": tab_words, "tab_scales": tab_scales,
        "offs": striped(np.random.permutation(T)[:S]),
        "pos1": striped(np.random.permutation(S)[:P]),
        "pos2": striped(np.random.permutation(S)[:P]),
        "w1": (n((K, H)) / np.sqrt(K) / s * u.T).astype(np.float32),
        "wear": np.random.uniform(0.4, 1.6, (H, S)).astype(np.float32),
        "gain": np.exp(0.3 * n(H)).astype(np.float32),
        "rest": (0.5 * n(H) * u[:, 0]).astype(np.float32),
        "lift": (0.6 * n(H) * u[:, 0]).astype(np.float32),
        "wr_words": wr_words, "wr_scales": wr_scales,
        "wp": (n((H, N)) / np.sqrt(H) / u).astype(np.float32),
        "br": (0.7 * n(N)).astype(np.float32),
    }

def reference(tab_words, tab_scales, offs, pos1, pos2, w1, wear, gain, rest, lift, wr_words, wr_scales, wp, br):
    v = unpack_weight(tab_words, tab_scales, "e4m3")[:, unstriped(offs)]
    h = (mxq(f64(w1), 0, "e4m3").T @ v) * f64(wear)
    h = h * f64(gain)[:, None]
    xa = np.maximum(h[:, unstriped(pos1)], f64(rest)[:, None])
    xb = np.abs(h[:, unstriped(pos2)]) + f64(lift)[:, None]
    wr = unpack_weight(wr_words, wr_scales, "e2m1")
    ya = wr.T @ mxq(xa, 0, "e4m3")
    yb = mxq(f64(wp), 0, "e4m3").T @ mxq(xb, 0, "e4m3")
    return (ya + f64(br)[:, None]) * yb

@@ -1,0 +1,305 @@
+from contextlib import ExitStack
+
+import concourse.mybir as mybir
+
+K, H, N, T, S, PICK = 1024, 1024, 512, 4096, 1024, 512
+FLOPS = 2 * K * H * S + 2 * 2 * H * N * PICK
+
+F32 = mybir.dt.float32
+BF16 = mybir.dt.bfloat16
+I32 = mybir.dt.int32
+U32 = mybir.dt.uint32
+U16 = mybir.dt.uint16
+U8 = mybir.dt.uint8
+FP8X4 = mybir.dt.float8_e4m3fn_x4
+FP4X4 = mybir.dt.float4_e2m1fn_x4
+ALU = mybir.AluOpType
+ACT = mybir.ActivationFunctionType
+
+P = 128
+PACK = 4
+PASS = P * PACK
+BANK = 512
+HALF = PICK // 2
+RUN = 4
+
+
+def tile_list_tremor_window_scores_kernel(
+    tc, tab_words, tab_scales, offs, pos1, pos2, w1, wear, gain, rest, lift, wr_words, wr_scales, wp, br, out
+):
+    nc = tc.nc
+    with ExitStack() as ctx:
+        lists = ctx.enter_context(tc.tile_pool(name="lists", bufs=1))
+        sb = ctx.enter_context(tc.tile_pool(name="sb", bufs=1))
+        psum = ctx.enter_context(tc.psum_pool(name="psum", bufs=1))
+
+        def tile(shape, dtype, tag, bufs=1):
+            return sb.tile(shape, dtype, name=tag, tag=tag, bufs=bufs, align_bytes=64)
+
+        def bank(tag, shape):
+            return psum.tile(shape, F32, name=tag, tag=tag)
+
+        offs_sb = lists.tile([P, S // 16], U16, name="offs_sb")
+        pos1_sb = lists.tile([P, PICK // 16], U16, name="pos1_sb")
+        pos2_sb = lists.tile([P, PICK // 16], U16, name="pos2_sb")
+
+        tab_planes = tile([P, T], U8, "tab_planes")
+        nc.vector.memset(tab_planes[:].bitcast(I32), 0)
+        for q in range(4):
+            nc.gpsimd.dma_start(
+                out=tab_planes[32 * q : 32 * q + 8, :].bitcast(I32),
+                in_=tab_scales[:, 4 * q : 4 * q + 4, :].bitcast(I32),
+            )
+        vecs = {}
+
+        def load_vec(name, vec):
+            vecs[name] = tile([P, 2, PACK], F32, name)
+            nc.sync.dma_start(out=vecs[name][:], in_=vec.rearrange("(b p t) -> p b t", b=2, t=PACK))
+
+        tab_sb = []
+
+        def load_tab(a):
+            tab_sb.append(tile([P, T], U32, "tab%d" % a))
+            nc.sync.dma_start(
+                out=tab_sb[a][:].bitcast(I32), in_=tab_words[a].rearrange("p t i -> p (t i)").bitcast(I32)
+            )
+
+        nc.sync.dma_start(offs_sb[:], offs)
+        load_tab(0)
+        load_vec("gain", gain)
+        nc.sync.dma_start(pos2_sb[:], pos2)
+        nc.sync.dma_start(pos1_sb[:], pos1)
+        load_tab(1)
+
+        def load_w1(a, b, u, parts):
+            width = PASS // parts
+            raw = tile([P, PACK, width], F32, "w1_raw_%d_%d_%d" % (a, b, u))
+            c0 = PASS * b + width * u
+            nc.sync.dma_start(
+                out=raw[:], in_=w1[PASS * a : PASS * (a + 1), c0 : c0 + width].rearrange("(p j) c -> p j c", j=PACK)
+            )
+            return raw
+
+        def load_wear(s):
+            b, t = divmod(s, PACK)
+            dst = tile([P, S], F32, "wear%d" % s)
+            rows = wear[PASS * b : PASS * (b + 1), :].rearrange("(p t) m -> p t m", t=PACK)
+            nc.sync.dma_start(out=dst[:], in_=rows[:, t, :])
+            return dst
+
+        def load_wp(b):
+            raw = tile([P, PACK, N], F32, "tab%d" % b)
+            nc.sync.dma_start(out=raw[:], in_=wp[PASS * b : PASS * (b + 1), :].rearrange("(p j) n -> p j n", j=PACK))
+            return raw
+
+        w1_raw = {(a, 0): [load_w1(a, 0, u, 2) for u in range(2)] for a in range(2)}
+        wear_sb = {0: load_wear(0)}
+        load_vec("lift", lift)
+        load_vec("rest", rest)
+        wear_sb[1] = load_wear(1)
+        for a in range(2):
+            w1_raw[(a, 1)] = [load_w1(a, 1, 0, 1)]
+        wear_sb[2] = load_wear(2)
+
+        v_planes = tile([P, S], U8, "v_planes")
+        nc.vector.tensor_copy(v_planes[:], tab_planes[:].indirect(offs_sb[:]))
+        v_words = []
+        for a in range(2):
+            v_words.append(tile([P, S], U32, "v_words%d" % a))
+            nc.vector.tensor_copy(v_words[a][:], tab_sb[a][:].indirect(offs_sb[:]))
+
+        wp_raw = {0: load_wp(0)}
+        wear_sb[3] = load_wear(3)
+        wp_raw[1] = load_wp(1)
+        for s in range(4, 8):
+            wear_sb[s] = load_wear(s)
+        wr_sb = tile([P, 2, 2 * N], U8, "wr")
+        nc.sync.dma_start(out=wr_sb[:].bitcast(I32), in_=wr_words.rearrange("a p n -> p a n").bitcast(I32))
+
+        wr_planes = tile([P, 2, N], U8, "wr_planes")
+        nc.gpsimd.memset(wr_planes[:].rearrange("p a n -> p (a n)").bitcast(I32), 0)
+        for q in range(4):
+            nc.sync.dma_start(
+                out=wr_planes[32 * q : 32 * q + 4, :, :].bitcast(I32),
+                in_=wr_scales[:, 4 * q : 4 * q + 4, :].rearrange("a r n -> r a n").bitcast(I32),
+            )
+        br_sb = tile([P, N // P], F32, "br")
+        with nc.allow_non_contiguous_dma(reason="one bias value for each output row"):
+            nc.sync.dma_start(out=br_sb[:], in_=br.rearrange("(c p) -> p c", p=P))
+
+        def quantize(src, width, tag):
+            codes = tile([P, width], U32, tag + "_codes")
+            planes = tile([P, width], U8, tag + "_planes")
+            nc.vector.quantize_mx(out=codes[:].bitcast(FP8X4), scales=planes[:], in_=src)
+            return codes, planes
+
+        def copy_on(engine, dst, src):
+            if engine == "vector":
+                nc.vector.tensor_copy(dst, src)
+            else:
+                nc.scalar.copy(dst, src)
+
+        def quantize_w1(a, b, engines):
+            grouped = tile([P, PACK, P, PACK], BF16, "w_grouped", bufs=2)
+            width = P // len(engines)
+            for u, engine in enumerate(engines):
+                copy_on(
+                    engine,
+                    grouped[:, :, width * u : width * (u + 1), :].rearrange("p t m j -> p m j t"),
+                    w1_raw[(a, b)][u][:].rearrange("p j (m t) -> p m j t", t=PACK),
+                )
+            return quantize(grouped[:].rearrange("p t m j -> p (t m j)"), PASS, "w1_%d_%d" % (a, b))
+
+        def interleave(dst, src):
+            nc.scalar.copy(
+                dst.rearrange("p (c i) t -> p c t i", i=RUN), src.rearrange("p t (c i) -> p c t i", i=RUN)
+            )
+
+        def quantize_wp(b):
+            grouped = tile([P, N, PACK], BF16, "w_grouped", bufs=2)
+            interleave(grouped[:], wp_raw[b][:])
+            return quantize(grouped[:].rearrange("p n j -> p (n j)"), N, "wp_%d" % b)
+
+        w1_q = {(a, 0): quantize_w1(a, 0, ("scalar", "vector")) for a in range(2)}
+
+        h_sb = {}
+
+        def first_stage(s):
+            b, t = divmod(s, PACK)
+            banks = [bank("h_bank%d" % (2 * (s % 2) + n), [P, BANK]) for n in range(2)]
+            for a in range(2):
+                codes, planes = w1_q[(a, b)]
+                for n in range(2):
+                    cols = slice(BANK * n, BANK * (n + 1))
+                    nc.tensor.matmul_mx(
+                        out=banks[n][:],
+                        lhsT=codes[:, P * t : P * (t + 1)].bitcast(FP8X4),
+                        lhsT_scale=planes[:, P * t : P * (t + 1)],
+                        rhs=v_words[a][:, cols].bitcast(FP8X4),
+                        rhs_scale=v_planes[4 * a :, cols],
+                        start=(a == 0),
+                        stop=(a == 1),
+                    )
+            h_sb[s] = tile([P, S], F32, "h", bufs=5)
+            for n in range(2):
+                cols = slice(BANK * n, BANK * (n + 1))
+                nc.vector.scalar_tensor_tensor(
+                    out=h_sb[s][:, cols],
+                    in0=banks[n][:],
+                    scalar=vecs["gain"][:, b, t : t + 1],
+                    in1=wear_sb[s][:, cols],
+                    op0=ALU.mult,
+                    op1=ALU.mult,
+                )
+
+        def posture_rows(s, xb_rows):
+            b, t = divmod(s, PACK)
+            picked = tile([P, PICK], F32, "picked_b", bufs=3)
+            nc.vector.tensor_copy(picked[:], h_sb[s][:].indirect(pos2_sb[:]))
+            size = tile([P, PICK], F32, "size_b", bufs=2)
+            nc.scalar.activation(size[:], picked[:], ACT.Abs)
+            nc.scalar.activation(xb_rows[:, t, :], size[:], ACT.Identity, bias=vecs["lift"][:, b, t : t + 1])
+
+        def rest_rows(s, xa_rows):
+            b, t = divmod(s, PACK)
+            picked = tile([P, PICK], F32, "picked_a", bufs=2)
+            nc.vector.tensor_copy(picked[:], h_sb[s][:].indirect(pos1_sb[:]))
+            nc.vector.tensor_scalar(
+                out=xa_rows[:, t, :], in0=picked[:], scalar1=vecs["rest"][:, b, t : t + 1], scalar2=None, op0=ALU.max
+            )
+
+        def second_stage(banks, b, half, moving, cols, stationary):
+            codes, planes = moving
+            for c in range(N // P):
+                lhs, lhs_scale = stationary(b, c)
+                nc.tensor.matmul_mx(
+                    out=banks[2 * half + c // 2][:, c % 2, :],
+                    lhsT=lhs,
+                    lhsT_scale=lhs_scale,
+                    rhs=codes[:, cols].bitcast(FP8X4),
+                    rhs_scale=planes[:, cols],
+                    start=(b == 0 and c % 2 == 0),
+                    stop=(b == 1 and c % 2 == 1),
+                )
+
+        wp_q = {}
+
+        def wp_side(b, c):
+            codes, planes = wp_q[b]
+            return codes[:, P * c : P * (c + 1)].bitcast(FP8X4), planes[:, P * c : P * (c + 1)]
+
+        def wr_side(b, c):
+            return wr_sb[:, b, 2 * P * c : 2 * P * (c + 1)].bitcast(FP4X4), wr_planes[:, b, P * c : P * (c + 1)]
+
+        halves = [slice(HALF * u, HALF * (u + 1)) for u in range(2)]
+
+        xa_rows = tile([P, PACK, PICK], BF16, "xa_rows")
+        xb_rows = tile([P, PACK, PICK], BF16, "xb_rows", bufs=2)
+        for s in range(PACK):
+            first_stage(s)
+            posture_rows(s, xb_rows)
+            rest_rows(s, xa_rows)
+            if s < 2:
+                w1_q[(s, 1)] = quantize_w1(s, 1, ("scalar",))
+            else:
+                wp_q[s - 2] = quantize_wp(s - 2)
+        xb_grouped = tile([P, PICK, PACK], BF16, "xb_grouped")
+        interleave(xb_grouped[:], xb_rows[:])
+        xb_q = quantize(xb_grouped[:].rearrange("p n j -> p (n j)"), PICK, "xb0")
+        xa_grouped = tile([P, PICK, PACK], BF16, "xa_grouped")
+        interleave(xa_grouped[:], xa_rows[:])
+        xa_q = quantize(xa_grouped[:].rearrange("p n j -> p (n j)"), PICK, "xa0")
+        yb_banks = [bank("yb_bank%d" % i, [P, 2, HALF]) for i in range(4)]
+        for u in range(2):
+            second_stage(yb_banks, 0, u, xb_q, halves[u], wp_side)
+
+        xb_rows = tile([P, PACK, PICK], BF16, "xb_rows", bufs=2)
+        for s in range(PACK, 2 * PACK):
+            first_stage(s)
+            posture_rows(s, xb_rows)
+        ya_banks = [bank("h_bank%d" % i, [P, 2, HALF]) for i in range(4)]
+        for u in range(2):
+            second_stage(ya_banks, 0, u, xa_q, halves[u], wr_side)
+
+        yb_sb = []
+        for u in range(2):
+            grouped = tile([P, HALF, PACK], BF16, "xb1_grouped%d" % u)
+            interleave(grouped[:], xb_rows[:, :, halves[u]])
+            xb_q = quantize(grouped[:].rearrange("p n j -> p (n j)"), HALF, "xb1_%d" % u)
+            second_stage(yb_banks, 1, u, xb_q, slice(0, HALF), wp_side)
+            yb_sb.append(tile([P, N // P, HALF], F32, "wear%d" % u))
+            for i in range(2):
+                nc.scalar.copy(yb_sb[u][:, 2 * i : 2 * i + 2, :], yb_banks[2 * u + i][:])
+
+        for u, held_by in enumerate(("wear7", "xb1_grouped1")):
+            picked = tile([P, PACK, HALF], F32, held_by)
+            for t in range(PACK):
+                nc.vector.tensor_copy(
+                    picked[:, t, :], h_sb[PACK + t][:].indirect(pos1_sb[:, HALF // 16 * u : HALF // 16 * (u + 1)])
+                )
+            grouped = tile([P, HALF, PACK], BF16, "xa1_grouped%d" % u)
+            nc.vector.tensor_tensor(
+                out=grouped[:].rearrange("p (c i) t -> p c t i", i=RUN),
+                in0=picked[:].rearrange("p t (c i) -> p c t i", i=RUN),
+                in1=vecs["rest"][:, 1, :].unsqueeze(1).unsqueeze(3).to_broadcast([P, HALF // RUN, PACK, RUN]),
+                op=ALU.max,
+            )
+            xa_q = quantize(grouped[:].rearrange("p n j -> p (n j)"), HALF, "xa1_%d" % u)
+            second_stage(ya_banks, 1, u, xa_q, slice(0, HALF), wr_side)
+
+        for u in range(2):
+            result = tile([P, N // P, HALF], F32, "wear%d" % (2 + u))
+            for c in range(N // P):
+                nc.vector.scalar_tensor_tensor(
+                    out=result[:, c, :],
+                    in0=ya_banks[2 * u + c // 2][:, c % 2, :],
+                    scalar=br_sb[:, c : c + 1],
+                    in1=yb_sb[u][:, c, :],
+                    op0=ALU.add,
+                    op1=ALU.mult,
+                )
+                if c % 2 == 1:
+                    nc.sync.dma_start(
+                        out=out[P * (c - 1) : P * (c + 1), halves[u]].rearrange("(c p) j -> p c j", p=P),
+                        in_=result[:, c - 1 : c + 1, :],
+                    )

@@ -45,31 +45,42 @@ def tile_list_tremor_window_scores_kernel(
 
         tab_planes = tile([P, T], U8, "tab_planes")
         nc.vector.memset(tab_planes[:].bitcast(I32), 0)
-        for q in range(4):
-            nc.gpsimd.dma_start(
-                out=tab_planes[32 * q : 32 * q + 8, :].bitcast(I32),
-                in_=tab_scales[:, 4 * q : 4 * q + 4, :].bitcast(I32),
-            )
         vecs = {}
 
         def load_vec(name, vec):
             vecs[name] = tile([P, 2, PACK], F32, name)
             nc.sync.dma_start(out=vecs[name][:], in_=vec.rearrange("(b p t) -> p b t", b=2, t=PACK))
 
-        tab_sb = []
+        tab_sb = [tile([P, T], U32, "tab%d" % a) for a in range(2)]
 
-        def load_tab(a):
-            tab_sb.append(tile([P, T], U32, "tab%d" % a))
+        def load_words(a, c0, c1):
+            words = tab_words[a].rearrange("p t i -> p (t i)").bitcast(I32)
+            nc.sync.dma_start(out=tab_sb[a][:, c0:c1].bitcast(I32), in_=words[:, c0:c1])
+
+        def load_scale_rows(a, q):
             nc.sync.dma_start(
-                out=tab_sb[a][:].bitcast(I32), in_=tab_words[a].rearrange("p t i -> p (t i)").bitcast(I32)
+                out=tab_planes[32 * q + 4 * a : 32 * q + 4 * a + 4, :].bitcast(I32),
+                in_=tab_scales[a, 4 * q : 4 * q + 4, :].bitcast(I32),
             )
 
+        br_sb = tile([P, N // P], F32, "br")
+        scale_rows = [(a, q) for q in range(4) for a in range(2)]
         nc.sync.dma_start(offs_sb[:], offs)
-        load_tab(0)
+        load_words(0, 0, 1536)
         load_vec("gain", gain)
         nc.sync.dma_start(pos2_sb[:], pos2)
         nc.sync.dma_start(pos1_sb[:], pos1)
-        load_tab(1)
+        load_vec("lift", lift)
+        load_vec("rest", rest)
+        with nc.allow_non_contiguous_dma(reason="one bias value for each output row"):
+            nc.sync.dma_start(out=br_sb[:], in_=br.rearrange("(c p) -> p c", p=P))
+        load_words(0, 1536, 3072)
+        for a, q in scale_rows[:6]:
+            load_scale_rows(a, q)
+        load_words(0, 3072, T)
+        for a, q in scale_rows[6:]:
+            load_scale_rows(a, q)
+        load_words(1, 0, T)
 
         def load_w1(a, b, u, parts):
             width = PASS // parts
@@ -88,25 +99,22 @@ def tile_list_tremor_window_scores_kernel(
             return dst
 
         def load_wp(b):
-            raw = tile([P, PACK, N], F32, "tab%d" % b)
+            raw = tile([P, PACK, N], F32, ("tab1", "tab_planes")[b])
             nc.sync.dma_start(out=raw[:], in_=wp[PASS * b : PASS * (b + 1), :].rearrange("(p j) n -> p j n", j=PACK))
             return raw
 
         w1_raw = {(a, 0): [load_w1(a, 0, u, 2) for u in range(2)] for a in range(2)}
         wear_sb = {0: load_wear(0)}
-        load_vec("lift", lift)
-        load_vec("rest", rest)
         wear_sb[1] = load_wear(1)
         for a in range(2):
             w1_raw[(a, 1)] = [load_w1(a, 1, 0, 1)]
         wear_sb[2] = load_wear(2)
 
-        v_planes = tile([P, S], U8, "v_planes")
+        v_words = [tile([P, S], U32, "v_words%d" % a) for a in range(2)]
+        nc.vector.tensor_copy(v_words[0][:], tab_sb[0][:].indirect(offs_sb[:]))
+        v_planes = tile([P, S], U8, "tab0")
         nc.vector.tensor_copy(v_planes[:], tab_planes[:].indirect(offs_sb[:]))
-        v_words = []
-        for a in range(2):
-            v_words.append(tile([P, S], U32, "v_words%d" % a))
-            nc.vector.tensor_copy(v_words[a][:], tab_sb[a][:].indirect(offs_sb[:]))
+        nc.vector.tensor_copy(v_words[1][:], tab_sb[1][:].indirect(offs_sb[:]))
 
         wp_raw = {0: load_wp(0)}
         wear_sb[3] = load_wear(3)
@@ -123,9 +131,6 @@ def tile_list_tremor_window_scores_kernel(
                 out=wr_planes[32 * q : 32 * q + 4, :, :].bitcast(I32),
                 in_=wr_scales[:, 4 * q : 4 * q + 4, :].rearrange("a r n -> r a n").bitcast(I32),
             )
-        br_sb = tile([P, N // P], F32, "br")
-        with nc.allow_non_contiguous_dma(reason="one bias value for each output row"):
-            nc.sync.dma_start(out=br_sb[:], in_=br.rearrange("(c p) -> p c", p=P))
 
         def quantize(src, width, tag):
             codes = tile([P, width], U32, tag + "_codes")
@@ -145,14 +150,14 @@ def tile_list_tremor_window_scores_kernel(
             for u, engine in enumerate(engines):
                 copy_on(
                     engine,
-                    grouped[:, :, width * u : width * (u + 1), :].rearrange("p t m j -> p m j t"),
-                    w1_raw[(a, b)][u][:].rearrange("p j (m t) -> p m j t", t=PACK),
+                    grouped[:, :, width * u : width * (u + 1), :].rearrange("p t m j -> p m t j"),
+                    w1_raw[(a, b)][u][:].rearrange("p j (m t) -> p m t j", t=PACK),
                 )
             return quantize(grouped[:].rearrange("p t m j -> p (t m j)"), PASS, "w1_%d_%d" % (a, b))
 
-        def interleave(dst, src):
-            nc.scalar.copy(
-                dst.rearrange("p (c i) t -> p c t i", i=RUN), src.rearrange("p t (c i) -> p c t i", i=RUN)
+        def interleave(dst, src, engine="scalar"):
+            copy_on(
+                engine, dst.rearrange("p (c i) t -> p c t i", i=RUN), src.rearrange("p t (c i) -> p c t i", i=RUN)
             )
 
         def quantize_wp(b):
@@ -277,13 +282,13 @@ def tile_list_tremor_window_scores_kernel(
                 nc.vector.tensor_copy(
                     picked[:, t, :], h_sb[PACK + t][:].indirect(pos1_sb[:, HALF // 16 * u : HALF // 16 * (u + 1)])
                 )
+            rows = tile([P, PACK, HALF], BF16, "xa1_rows%d" % u)
+            for t in range(PACK):
+                nc.vector.tensor_scalar(
+                    out=rows[:, t, :], in0=picked[:, t, :], scalar1=vecs["rest"][:, 1, t : t + 1], scalar2=None, op0=ALU.max
+                )
             grouped = tile([P, HALF, PACK], BF16, "xa1_grouped%d" % u)
-            nc.vector.tensor_tensor(
-                out=grouped[:].rearrange("p (c i) t -> p c t i", i=RUN),
-                in0=picked[:].rearrange("p t (c i) -> p c t i", i=RUN),
-                in1=vecs["rest"][:, 1, :].unsqueeze(1).unsqueeze(3).to_broadcast([P, HALF // RUN, PACK, RUN]),
-                op=ALU.max,
-            )
+            interleave(grouped[:], rows[:], "vector")
             xa_q = quantize(grouped[:].rearrange("p n j -> p (n j)"), HALF, "xa1_%d" % u)
             second_stage(ya_banks, 1, u, xa_q, slice(0, HALF), wr_side)
 

@@ -22,6 +22,7 @@ PASS = P * PACK
 BANK = 512
 HALF = PICK // 2
 RUN = 4
+F32_MAX = 3.4028234663852886e38
 
 
 def tile_list_tremor_window_scores_kernel(
@@ -132,10 +133,13 @@ def tile_list_tremor_window_scores_kernel(
                 in_=wr_scales[:, 4 * q : 4 * q + 4, :].rearrange("a r n -> r a n").bitcast(I32),
             )
 
-        def quantize(src, width, tag):
+        def quantize(src, width, tag, cuts=()):
             codes = tile([P, width], U32, tag + "_codes")
             planes = tile([P, width], U8, tag + "_planes")
-            nc.vector.quantize_mx(out=codes[:].bitcast(FP8X4), scales=planes[:], in_=src)
+            for c0, c1 in zip((0, *cuts), (*cuts, width)):
+                nc.vector.quantize_mx(
+                    out=codes[:, c0:c1].bitcast(FP8X4), scales=planes[:, c0:c1], in_=src[:, PACK * c0 : PACK * c1]
+                )
             return codes, planes
 
         def copy_on(engine, dst, src):
@@ -144,7 +148,7 @@ def tile_list_tremor_window_scores_kernel(
             else:
                 nc.scalar.copy(dst, src)
 
-        def quantize_w1(a, b, engines):
+        def quantize_w1(a, b, engines, cuts=()):
             grouped = tile([P, PACK, P, PACK], BF16, "w_grouped", bufs=2)
             width = P // len(engines)
             for u, engine in enumerate(engines):
@@ -153,7 +157,7 @@ def tile_list_tremor_window_scores_kernel(
                     grouped[:, :, width * u : width * (u + 1), :].rearrange("p t m j -> p m t j"),
                     w1_raw[(a, b)][u][:].rearrange("p j (m t) -> p m t j", t=PACK),
                 )
-            return quantize(grouped[:].rearrange("p t m j -> p (t m j)"), PASS, "w1_%d_%d" % (a, b))
+            return quantize(grouped[:].rearrange("p t m j -> p (t m j)"), PASS, "w1_%d_%d" % (a, b), cuts)
 
         def interleave(dst, src, engine="scalar"):
             copy_on(
@@ -165,7 +169,8 @@ def tile_list_tremor_window_scores_kernel(
             interleave(grouped[:], wp_raw[b][:])
             return quantize(grouped[:].rearrange("p n j -> p (n j)"), N, "wp_%d" % b)
 
-        w1_q = {(a, 0): quantize_w1(a, 0, ("scalar", "vector")) for a in range(2)}
+        w1_q = {(0, 0): quantize_w1(0, 0, ("scalar", "vector"))}
+        w1_q[(1, 0)] = quantize_w1(1, 0, ("scalar", "vector"), cuts=(P,))
 
         h_sb = {}
 
@@ -203,14 +208,26 @@ def tile_list_tremor_window_scores_kernel(
             nc.vector.tensor_copy(picked[:], h_sb[s][:].indirect(pos2_sb[:]))
             size = tile([P, PICK], F32, "size_b", bufs=2)
             nc.scalar.activation(size[:], picked[:], ACT.Abs)
-            nc.scalar.activation(xb_rows[:, t, :], size[:], ACT.Identity, bias=vecs["lift"][:, b, t : t + 1])
+            nc.gpsimd.tensor_scalar(
+                out=xb_rows[:, t, :],
+                in0=size[:],
+                scalar1=1.0,
+                scalar2=vecs["lift"][:, b, t : t + 1],
+                op0=ALU.mult,
+                op1=ALU.add,
+            )
 
         def rest_rows(s, xa_rows):
             b, t = divmod(s, PACK)
             picked = tile([P, PICK], F32, "picked_a", bufs=2)
             nc.vector.tensor_copy(picked[:], h_sb[s][:].indirect(pos1_sb[:]))
-            nc.vector.tensor_scalar(
-                out=xa_rows[:, t, :], in0=picked[:], scalar1=vecs["rest"][:, b, t : t + 1], scalar2=None, op0=ALU.max
+            nc.gpsimd.tensor_scalar(
+                out=xa_rows[:, t, :],
+                in0=picked[:],
+                scalar1=F32_MAX,
+                scalar2=vecs["rest"][:, b, t : t + 1],
+                op0=ALU.min,
+                op1=ALU.max,
             )
 
         def second_stage(banks, b, half, moving, cols, stationary):
@@ -242,8 +259,8 @@ def tile_list_tremor_window_scores_kernel(
         xb_rows = tile([P, PACK, PICK], BF16, "xb_rows", bufs=2)
         for s in range(PACK):
             first_stage(s)
-            posture_rows(s, xb_rows)
             rest_rows(s, xa_rows)
+            posture_rows(s, xb_rows)
             if s < 2:
                 w1_q[(s, 1)] = quantize_w1(s, 1, ("scalar",))
             else:

@@ -22,7 +22,6 @@ PASS = P * PACK
 BANK = 512
 HALF = PICK // 2
 RUN = 4
-F32_MAX = 3.4028234663852886e38
 
 
 def tile_list_tremor_window_scores_kernel(
@@ -64,24 +63,21 @@ def tile_list_tremor_window_scores_kernel(
                 in_=tab_scales[a, 4 * q : 4 * q + 4, :].bitcast(I32),
             )
 
-        br_sb = tile([P, N // P], F32, "br")
         scale_rows = [(a, q) for q in range(4) for a in range(2)]
         nc.sync.dma_start(offs_sb[:], offs)
-        load_words(0, 0, 1536)
+        load_words(0, 0, 768)
+        load_words(0, 768, 1536)
         load_vec("gain", gain)
         nc.sync.dma_start(pos2_sb[:], pos2)
         nc.sync.dma_start(pos1_sb[:], pos1)
         load_vec("lift", lift)
         load_vec("rest", rest)
-        with nc.allow_non_contiguous_dma(reason="one bias value for each output row"):
-            nc.sync.dma_start(out=br_sb[:], in_=br.rearrange("(c p) -> p c", p=P))
         load_words(0, 1536, 3072)
         for a, q in scale_rows[:6]:
             load_scale_rows(a, q)
         load_words(0, 3072, T)
         for a, q in scale_rows[6:]:
             load_scale_rows(a, q)
-        load_words(1, 0, T)
 
         def load_w1(a, b, u, parts):
             width = PASS // parts
@@ -104,12 +100,15 @@ def tile_list_tremor_window_scores_kernel(
             nc.sync.dma_start(out=raw[:], in_=wp[PASS * b : PASS * (b + 1), :].rearrange("(p j) n -> p j n", j=PACK))
             return raw
 
-        w1_raw = {(a, 0): [load_w1(a, 0, u, 2) for u in range(2)] for a in range(2)}
+        w1_raw = {(0, 0): [load_w1(0, 0, 0, 1)]}
+        load_words(1, 0, T)
+        w1_raw[(1, 0)] = [load_w1(1, 0, u, 2) for u in range(2)]
         wear_sb = {0: load_wear(0)}
-        wear_sb[1] = load_wear(1)
-        for a in range(2):
-            w1_raw[(a, 1)] = [load_w1(a, 1, 0, 1)]
-        wear_sb[2] = load_wear(2)
+        for s in (1, 2):
+            wear_sb[s] = load_wear(s)
+        w1_raw[(0, 1)] = [load_w1(0, 1, 0, 1)]
+        wear_sb[3] = load_wear(3)
+        w1_raw[(1, 1)] = [load_w1(1, 1, 0, 1)]
 
         v_words = [tile([P, S], U32, "v_words%d" % a) for a in range(2)]
         nc.vector.tensor_copy(v_words[0][:], tab_sb[0][:].indirect(offs_sb[:]))
@@ -117,11 +116,11 @@ def tile_list_tremor_window_scores_kernel(
         nc.vector.tensor_copy(v_planes[:], tab_planes[:].indirect(offs_sb[:]))
         nc.vector.tensor_copy(v_words[1][:], tab_sb[1][:].indirect(offs_sb[:]))
 
-        wp_raw = {0: load_wp(0)}
-        wear_sb[3] = load_wear(3)
-        wp_raw[1] = load_wp(1)
-        for s in range(4, 8):
-            wear_sb[s] = load_wear(s)
+        wp_raw = {}
+        for b in range(2):
+            wp_raw[b] = load_wp(b)
+            for s in (4 + 2 * b, 5 + 2 * b):
+                wear_sb[s] = load_wear(s)
         wr_sb = tile([P, 2, 2 * N], U8, "wr")
         nc.sync.dma_start(out=wr_sb[:].bitcast(I32), in_=wr_words.rearrange("a p n -> p a n").bitcast(I32))
 
@@ -132,6 +131,9 @@ def tile_list_tremor_window_scores_kernel(
                 out=wr_planes[32 * q : 32 * q + 4, :, :].bitcast(I32),
                 in_=wr_scales[:, 4 * q : 4 * q + 4, :].rearrange("a r n -> r a n").bitcast(I32),
             )
+        br_sb = tile([P, N // P], F32, "br")
+        with nc.allow_non_contiguous_dma(reason="one bias value for each output row"):
+            nc.sync.dma_start(out=br_sb[:], in_=br.rearrange("(c p) -> p c", p=P))
 
         def quantize(src, width, tag, cuts=()):
             codes = tile([P, width], U32, tag + "_codes")
@@ -149,7 +151,7 @@ def tile_list_tremor_window_scores_kernel(
                 nc.scalar.copy(dst, src)
 
         def quantize_w1(a, b, engines, cuts=()):
-            grouped = tile([P, PACK, P, PACK], BF16, "w_grouped", bufs=2)
+            grouped = tile([P, PACK, P, PACK], BF16, "w1_grouped%d" % a)
             width = P // len(engines)
             for u, engine in enumerate(engines):
                 copy_on(
@@ -165,11 +167,11 @@ def tile_list_tremor_window_scores_kernel(
             )
 
         def quantize_wp(b):
-            grouped = tile([P, N, PACK], BF16, "w_grouped", bufs=2)
+            grouped = tile([P, N, PACK], BF16, "wp_grouped", bufs=2)
             interleave(grouped[:], wp_raw[b][:])
             return quantize(grouped[:].rearrange("p n j -> p (n j)"), N, "wp_%d" % b)
 
-        w1_q = {(0, 0): quantize_w1(0, 0, ("scalar", "vector"))}
+        w1_q = {(0, 0): quantize_w1(0, 0, ("scalar",))}
         w1_q[(1, 0)] = quantize_w1(1, 0, ("scalar", "vector"), cuts=(P,))
 
         h_sb = {}
@@ -190,7 +192,7 @@ def tile_list_tremor_window_scores_kernel(
                         start=(a == 0),
                         stop=(a == 1),
                     )
-            h_sb[s] = tile([P, S], F32, "h", bufs=5)
+            h_sb[s] = tile([P, S], F32, "h", bufs=6)
             for n in range(2):
                 cols = slice(BANK * n, BANK * (n + 1))
                 nc.vector.scalar_tensor_tensor(
@@ -204,30 +206,24 @@ def tile_list_tremor_window_scores_kernel(
 
         def posture_rows(s, xb_rows):
             b, t = divmod(s, PACK)
-            picked = tile([P, PICK], F32, "picked_b", bufs=3)
+            picked = tile([P, PICK], F32, "picked_b", bufs=5)
             nc.vector.tensor_copy(picked[:], h_sb[s][:].indirect(pos2_sb[:]))
             size = tile([P, PICK], F32, "size_b", bufs=2)
             nc.scalar.activation(size[:], picked[:], ACT.Abs)
-            nc.gpsimd.tensor_scalar(
-                out=xb_rows[:, t, :],
-                in0=size[:],
-                scalar1=1.0,
-                scalar2=vecs["lift"][:, b, t : t + 1],
-                op0=ALU.mult,
-                op1=ALU.add,
-            )
+            nc.scalar.activation(xb_rows[:, t, :], size[:], ACT.Identity, bias=vecs["lift"][:, b, t : t + 1])
 
-        def rest_rows(s, xa_rows):
-            b, t = divmod(s, PACK)
-            picked = tile([P, PICK], F32, "picked_a", bufs=2)
+        def pick_rest(s):
+            if s == PACK - 1:
+                picked = tile([P, PICK], F32, "w1_grouped1")
+            else:
+                picked = tile([P, PICK], F32, "picked_a", bufs=2)
             nc.vector.tensor_copy(picked[:], h_sb[s][:].indirect(pos1_sb[:]))
-            nc.gpsimd.tensor_scalar(
-                out=xa_rows[:, t, :],
-                in0=picked[:],
-                scalar1=F32_MAX,
-                scalar2=vecs["rest"][:, b, t : t + 1],
-                op0=ALU.min,
-                op1=ALU.max,
+            return picked
+
+        def floor_rows(dst, picked, s):
+            b, t = divmod(s, PACK)
+            nc.vector.tensor_scalar(
+                out=dst, in0=picked, scalar1=vecs["rest"][:, b, t : t + 1], scalar2=None, op0=ALU.max
             )
 
         def second_stage(banks, b, half, moving, cols, stationary):
@@ -257,14 +253,18 @@ def tile_list_tremor_window_scores_kernel(
 
         xa_rows = tile([P, PACK, PICK], BF16, "xa_rows")
         xb_rows = tile([P, PACK, PICK], BF16, "xb_rows", bufs=2)
+        first_stage(0)
+        picked_a = {}
         for s in range(PACK):
-            first_stage(s)
-            rest_rows(s, xa_rows)
+            if s in (1, 2):
+                w1_q[(s - 1, 1)] = quantize_w1(s - 1, 1, ("scalar",))
+            first_stage(s + 1)
             posture_rows(s, xb_rows)
-            if s < 2:
-                w1_q[(s, 1)] = quantize_w1(s, 1, ("scalar",))
-            else:
-                wp_q[s - 2] = quantize_wp(s - 2)
+            if s > 0:
+                floor_rows(xa_rows[:, s - 1, :], picked_a[s - 1][:], s - 1)
+            picked_a[s] = pick_rest(s)
+        wp_q[0] = quantize_wp(0)
+        floor_rows(xa_rows[:, PACK - 1, :], picked_a[PACK - 1][:], PACK - 1)
         xb_grouped = tile([P, PICK, PACK], BF16, "xb_grouped")
         interleave(xb_grouped[:], xb_rows[:])
         xb_q = quantize(xb_grouped[:].rearrange("p n j -> p (n j)"), PICK, "xb0")
@@ -277,8 +277,11 @@ def tile_list_tremor_window_scores_kernel(
 
         xb_rows = tile([P, PACK, PICK], BF16, "xb_rows", bufs=2)
         for s in range(PACK, 2 * PACK):
-            first_stage(s)
+            if s + 1 < 2 * PACK:
+                first_stage(s + 1)
             posture_rows(s, xb_rows)
+            if s == PACK:
+                wp_q[1] = quantize_wp(1)
         ya_banks = [bank("h_bank%d" % i, [P, 2, HALF]) for i in range(4)]
         for u in range(2):
             second_stage(ya_banks, 0, u, xa_q, halves[u], wr_side)
@@ -293,7 +296,7 @@ def tile_list_tremor_window_scores_kernel(
             for i in range(2):
                 nc.scalar.copy(yb_sb[u][:, 2 * i : 2 * i + 2, :], yb_banks[2 * u + i][:])
 
-        for u, held_by in enumerate(("wear7", "xb1_grouped1")):
+        for u, held_by in enumerate(("wear7", "xb1_grouped0")):
             picked = tile([P, PACK, HALF], F32, held_by)
             for t in range(PACK):
                 nc.vector.tensor_copy(
@@ -301,9 +304,7 @@ def tile_list_tremor_window_scores_kernel(
                 )
             rows = tile([P, PACK, HALF], BF16, "xa1_rows%d" % u)
             for t in range(PACK):
-                nc.vector.tensor_scalar(
-                    out=rows[:, t, :], in0=picked[:, t, :], scalar1=vecs["rest"][:, 1, t : t + 1], scalar2=None, op0=ALU.max
-                )
+                floor_rows(rows[:, t, :], picked[:, t, :], PACK + t)
             grouped = tile([P, HALF, PACK], BF16, "xa1_grouped%d" % u)
             interleave(grouped[:], rows[:], "vector")
             xa_q = quantize(grouped[:].rearrange("p n j -> p (n j)"), HALF, "xa1_%d" % u)
@@ -320,8 +321,5 @@ def tile_list_tremor_window_scores_kernel(
                     op0=ALU.add,
                     op1=ALU.mult,
                 )
-                if c % 2 == 1:
-                    nc.sync.dma_start(
-                        out=out[P * (c - 1) : P * (c + 1), halves[u]].rearrange("(c p) j -> p c j", p=P),
-                        in_=result[:, c - 1 : c + 1, :],
-                    )
+                queue = nc.scalar if c % 2 == 0 else nc.sync
+                queue.dma_start(out=out[P * c : P * (c + 1), halves[u]], in_=result[:, c, :])

@@ -20,7 +20,6 @@ P = 128
 PACK = 4
 PASS = P * PACK
 BANK = 512
-HALF = PICK // 2
 RUN = 4
 
 
@@ -57,27 +56,24 @@ def tile_list_tremor_window_scores_kernel(
             words = tab_words[a].rearrange("p t i -> p (t i)").bitcast(I32)
             nc.sync.dma_start(out=tab_sb[a][:, c0:c1].bitcast(I32), in_=words[:, c0:c1])
 
-        def load_scale_rows(a, q):
+        def load_scale_rows(a, r):
             nc.sync.dma_start(
-                out=tab_planes[32 * q + 4 * a : 32 * q + 4 * a + 4, :].bitcast(I32),
-                in_=tab_scales[a, 4 * q : 4 * q + 4, :].bitcast(I32),
+                out=tab_planes[4 * a + r : P : 32, :].bitcast(I32),
+                in_=tab_scales[a].rearrange("(q r) t -> r q t", r=4)[r].bitcast(I32),
             )
 
-        scale_rows = [(a, q) for q in range(4) for a in range(2)]
+        scale_rows = [(a, r) for r in range(4) for a in range(2)]
         nc.sync.dma_start(offs_sb[:], offs)
-        load_words(0, 0, 768)
-        load_words(0, 768, 1536)
+        load_words(0, 0, 1280)
+        load_words(0, 1280, 2560)
         load_vec("gain", gain)
         nc.sync.dma_start(pos2_sb[:], pos2)
         nc.sync.dma_start(pos1_sb[:], pos1)
         load_vec("lift", lift)
         load_vec("rest", rest)
-        load_words(0, 1536, 3072)
-        for a, q in scale_rows[:6]:
-            load_scale_rows(a, q)
-        load_words(0, 3072, T)
-        for a, q in scale_rows[6:]:
-            load_scale_rows(a, q)
+        load_words(0, 2560, T)
+        for a, r in scale_rows[:6]:
+            load_scale_rows(a, r)
 
         def load_w1(a, b, u, parts):
             width = PASS // parts
@@ -101,6 +97,8 @@ def tile_list_tremor_window_scores_kernel(
             return raw
 
         w1_raw = {(0, 0): [load_w1(0, 0, 0, 1)]}
+        for a, r in scale_rows[6:]:
+            load_scale_rows(a, r)
         load_words(1, 0, T)
         w1_raw[(1, 0)] = [load_w1(1, 0, u, 2) for u in range(2)]
         wear_sb = {0: load_wear(0)}
@@ -226,18 +224,18 @@ def tile_list_tremor_window_scores_kernel(
                 out=dst, in0=picked, scalar1=vecs["rest"][:, b, t : t + 1], scalar2=None, op0=ALU.max
             )
 
-        def second_stage(banks, b, half, moving, cols, stationary):
+        def second_stage(banks, b, moving, stationary):
             codes, planes = moving
             for c in range(N // P):
                 lhs, lhs_scale = stationary(b, c)
                 nc.tensor.matmul_mx(
-                    out=banks[2 * half + c // 2][:, c % 2, :],
+                    out=banks[c][:],
                     lhsT=lhs,
                     lhsT_scale=lhs_scale,
-                    rhs=codes[:, cols].bitcast(FP8X4),
-                    rhs_scale=planes[:, cols],
-                    start=(b == 0 and c % 2 == 0),
-                    stop=(b == 1 and c % 2 == 1),
+                    rhs=codes[:].bitcast(FP8X4),
+                    rhs_scale=planes[:],
+                    start=(b == 0),
+                    stop=(b == 1),
                 )
 
         wp_q = {}
@@ -248,8 +246,6 @@ def tile_list_tremor_window_scores_kernel(
 
         def wr_side(b, c):
             return wr_sb[:, b, 2 * P * c : 2 * P * (c + 1)].bitcast(FP4X4), wr_planes[:, b, P * c : P * (c + 1)]
-
-        halves = [slice(HALF * u, HALF * (u + 1)) for u in range(2)]
 
         xa_rows = tile([P, PACK, PICK], BF16, "xa_rows")
         xb_rows = tile([P, PACK, PICK], BF16, "xb_rows", bufs=2)
@@ -271,9 +267,8 @@ def tile_list_tremor_window_scores_kernel(
         xa_grouped = tile([P, PICK, PACK], BF16, "xa_grouped")
         interleave(xa_grouped[:], xa_rows[:])
         xa_q = quantize(xa_grouped[:].rearrange("p n j -> p (n j)"), PICK, "xa0")
-        yb_banks = [bank("yb_bank%d" % i, [P, 2, HALF]) for i in range(4)]
-        for u in range(2):
-            second_stage(yb_banks, 0, u, xb_q, halves[u], wp_side)
+        yb_banks = [bank("yb_bank%d" % c, [P, PICK]) for c in range(N // P)]
+        second_stage(yb_banks, 0, xb_q, wp_side)
 
         xb_rows = tile([P, PACK, PICK], BF16, "xb_rows", bufs=2)
         for s in range(PACK, 2 * PACK):
@@ -282,44 +277,38 @@ def tile_list_tremor_window_scores_kernel(
             posture_rows(s, xb_rows)
             if s == PACK:
                 wp_q[1] = quantize_wp(1)
-        ya_banks = [bank("h_bank%d" % i, [P, 2, HALF]) for i in range(4)]
-        for u in range(2):
-            second_stage(ya_banks, 0, u, xa_q, halves[u], wr_side)
+        ya_banks = [bank("h_bank%d" % c, [P, PICK]) for c in range(N // P)]
+        second_stage(ya_banks, 0, xa_q, wr_side)
 
+        xb_grouped = tile([P, PICK, PACK], BF16, "xb_grouped")
+        interleave(xb_grouped[:], xb_rows[:])
+        xb_q = quantize(xb_grouped[:].rearrange("p n j -> p (n j)"), PICK, "xb1")
+        second_stage(yb_banks, 1, xb_q, wp_side)
         yb_sb = []
-        for u in range(2):
-            grouped = tile([P, HALF, PACK], BF16, "xb1_grouped%d" % u)
-            interleave(grouped[:], xb_rows[:, :, halves[u]])
-            xb_q = quantize(grouped[:].rearrange("p n j -> p (n j)"), HALF, "xb1_%d" % u)
-            second_stage(yb_banks, 1, u, xb_q, slice(0, HALF), wp_side)
-            yb_sb.append(tile([P, N // P, HALF], F32, "wear%d" % u))
-            for i in range(2):
-                nc.scalar.copy(yb_sb[u][:, 2 * i : 2 * i + 2, :], yb_banks[2 * u + i][:])
+        for c in range(N // P):
+            yb_sb.append(tile([P, PICK], F32, "wear%d" % c))
+            nc.scalar.copy(yb_sb[c][:], yb_banks[c][:])
 
-        for u, held_by in enumerate(("wear7", "xb1_grouped0")):
-            picked = tile([P, PACK, HALF], F32, held_by)
-            for t in range(PACK):
-                nc.vector.tensor_copy(
-                    picked[:, t, :], h_sb[PACK + t][:].indirect(pos1_sb[:, HALF // 16 * u : HALF // 16 * (u + 1)])
-                )
-            rows = tile([P, PACK, HALF], BF16, "xa1_rows%d" % u)
-            for t in range(PACK):
-                floor_rows(rows[:, t, :], picked[:, t, :], PACK + t)
-            grouped = tile([P, HALF, PACK], BF16, "xa1_grouped%d" % u)
-            interleave(grouped[:], rows[:], "vector")
-            xa_q = quantize(grouped[:].rearrange("p n j -> p (n j)"), HALF, "xa1_%d" % u)
-            second_stage(ya_banks, 1, u, xa_q, slice(0, HALF), wr_side)
+        picked = tile([P, PACK, PICK], F32, "wear7")
+        xa_rows = tile([P, PACK, PICK], BF16, "xa_rows")
+        for t in range(PACK):
+            nc.vector.tensor_copy(picked[:, t, :], h_sb[PACK + t][:].indirect(pos1_sb[:]))
+        for t in range(PACK):
+            floor_rows(xa_rows[:, t, :], picked[:, t, :], PACK + t)
+        xa_grouped = tile([P, PICK, PACK], BF16, "xb_grouped")
+        interleave(xa_grouped[:], xa_rows[:], "vector")
+        xa_q = quantize(xa_grouped[:].rearrange("p n j -> p (n j)"), PICK, "xa1")
+        second_stage(ya_banks, 1, xa_q, wr_side)
 
-        for u in range(2):
-            result = tile([P, N // P, HALF], F32, "wear%d" % (2 + u))
-            for c in range(N // P):
-                nc.vector.scalar_tensor_tensor(
-                    out=result[:, c, :],
-                    in0=ya_banks[2 * u + c // 2][:, c % 2, :],
-                    scalar=br_sb[:, c : c + 1],
-                    in1=yb_sb[u][:, c, :],
-                    op0=ALU.add,
-                    op1=ALU.mult,
-                )
-                queue = nc.scalar if c % 2 == 0 else nc.sync
-                queue.dma_start(out=out[P * c : P * (c + 1), halves[u]], in_=result[:, c, :])
+        for c in range(N // P):
+            result = tile([P, PICK], F32, "result", bufs=N // P)
+            nc.vector.scalar_tensor_tensor(
+                out=result[:],
+                in0=ya_banks[c][:],
+                scalar=br_sb[:, c : c + 1],
+                in1=yb_sb[c][:],
+                op0=ALU.add,
+                op1=ALU.mult,
+            )
+            queue = nc.scalar if c % 2 == 0 else nc.sync
+            queue.dma_start(out=out[P * c : P * (c + 1), :], in_=result[:])

from contextlib import ExitStack

import concourse.mybir as mybir

K, H, N, T, S, PICK = 1024, 1024, 512, 4096, 1024, 512
FLOPS = 2 * K * H * S + 2 * 2 * H * N * PICK

F32 = mybir.dt.float32
BF16 = mybir.dt.bfloat16
I32 = mybir.dt.int32
U32 = mybir.dt.uint32
U16 = mybir.dt.uint16
U8 = mybir.dt.uint8
FP8X4 = mybir.dt.float8_e4m3fn_x4
FP4X4 = mybir.dt.float4_e2m1fn_x4
ALU = mybir.AluOpType
ACT = mybir.ActivationFunctionType

P = 128
PACK = 4
PASS = P * PACK
BANK = 512
RUN = 4


def tile_list_tremor_window_scores_kernel(
    tc, tab_words, tab_scales, offs, pos1, pos2, w1, wear, gain, rest, lift, wr_words, wr_scales, wp, br, out
):
    nc = tc.nc
    with ExitStack() as ctx:
        lists = ctx.enter_context(tc.tile_pool(name="lists", bufs=1))
        sb = ctx.enter_context(tc.tile_pool(name="sb", bufs=1))
        psum = ctx.enter_context(tc.psum_pool(name="psum", bufs=1))

        def tile(shape, dtype, tag, bufs=1):
            return sb.tile(shape, dtype, name=tag, tag=tag, bufs=bufs, align_bytes=64)

        def bank(tag, shape):
            return psum.tile(shape, F32, name=tag, tag=tag)

        offs_sb = lists.tile([P, S // 16], U16, name="offs_sb")
        pos1_sb = lists.tile([P, PICK // 16], U16, name="pos1_sb")
        pos2_sb = lists.tile([P, PICK // 16], U16, name="pos2_sb")

        tab_planes = tile([P, T], U8, "tab_planes")
        nc.vector.memset(tab_planes[:].bitcast(I32), 0)
        vecs = {}

        def load_vec(name, vec):
            vecs[name] = tile([P, 2, PACK], F32, name)
            nc.sync.dma_start(out=vecs[name][:], in_=vec.rearrange("(b p t) -> p b t", b=2, t=PACK))

        tab_sb = [tile([P, T], U32, "tab%d" % a) for a in range(2)]

        def load_words(a, c0, c1):
            words = tab_words[a].rearrange("p t i -> p (t i)").bitcast(I32)
            nc.sync.dma_start(out=tab_sb[a][:, c0:c1].bitcast(I32), in_=words[:, c0:c1])

        def load_scale_rows(a, r):
            nc.sync.dma_start(
                out=tab_planes[4 * a + r : P : 32, :].bitcast(I32),
                in_=tab_scales[a].rearrange("(q r) t -> r q t", r=4)[r].bitcast(I32),
            )

        scale_rows = [(a, r) for r in range(4) for a in range(2)]
        nc.sync.dma_start(offs_sb[:], offs)
        load_words(0, 0, 1280)
        load_words(0, 1280, 2560)
        load_vec("gain", gain)
        nc.sync.dma_start(pos2_sb[:], pos2)
        nc.sync.dma_start(pos1_sb[:], pos1)
        load_vec("lift", lift)
        load_vec("rest", rest)
        load_words(0, 2560, T)
        for a, r in scale_rows[:6]:
            load_scale_rows(a, r)

        def load_w1(a, b, u, parts):
            width = PASS // parts
            raw = tile([P, PACK, width], F32, "w1_raw_%d_%d_%d" % (a, b, u))
            c0 = PASS * b + width * u
            nc.sync.dma_start(
                out=raw[:], in_=w1[PASS * a : PASS * (a + 1), c0 : c0 + width].rearrange("(p j) c -> p j c", j=PACK)
            )
            return raw

        def load_wear(s):
            b, t = divmod(s, PACK)
            dst = tile([P, S], F32, "wear%d" % s)
            rows = wear[PASS * b : PASS * (b + 1), :].rearrange("(p t) m -> p t m", t=PACK)
            nc.sync.dma_start(out=dst[:], in_=rows[:, t, :])
            return dst

        def load_wp(b):
            raw = tile([P, PACK, N], F32, ("tab1", "tab_planes")[b])
            nc.sync.dma_start(out=raw[:], in_=wp[PASS * b : PASS * (b + 1), :].rearrange("(p j) n -> p j n", j=PACK))
            return raw

        w1_raw = {(0, 0): [load_w1(0, 0, 0, 1)]}
        for a, r in scale_rows[6:]:
            load_scale_rows(a, r)
        load_words(1, 0, T)
        w1_raw[(1, 0)] = [load_w1(1, 0, u, 2) for u in range(2)]
        wear_sb = {0: load_wear(0)}
        for s in (1, 2):
            wear_sb[s] = load_wear(s)
        w1_raw[(0, 1)] = [load_w1(0, 1, 0, 1)]
        wear_sb[3] = load_wear(3)
        w1_raw[(1, 1)] = [load_w1(1, 1, 0, 1)]

        v_words = [tile([P, S], U32, "v_words%d" % a) for a in range(2)]
        nc.vector.tensor_copy(v_words[0][:], tab_sb[0][:].indirect(offs_sb[:]))
        v_planes = tile([P, S], U8, "tab0")
        nc.vector.tensor_copy(v_planes[:], tab_planes[:].indirect(offs_sb[:]))
        nc.vector.tensor_copy(v_words[1][:], tab_sb[1][:].indirect(offs_sb[:]))

        wp_raw = {}
        for b in range(2):
            wp_raw[b] = load_wp(b)
            for s in (4 + 2 * b, 5 + 2 * b):
                wear_sb[s] = load_wear(s)
        wr_sb = tile([P, 2, 2 * N], U8, "wr")
        nc.sync.dma_start(out=wr_sb[:].bitcast(I32), in_=wr_words.rearrange("a p n -> p a n").bitcast(I32))

        wr_planes = tile([P, 2, N], U8, "wr_planes")
        nc.gpsimd.memset(wr_planes[:].rearrange("p a n -> p (a n)").bitcast(I32), 0)
        for q in range(4):
            nc.sync.dma_start(
                out=wr_planes[32 * q : 32 * q + 4, :, :].bitcast(I32),
                in_=wr_scales[:, 4 * q : 4 * q + 4, :].rearrange("a r n -> r a n").bitcast(I32),
            )
        br_sb = tile([P, N // P], F32, "br")
        with nc.allow_non_contiguous_dma(reason="one bias value for each output row"):
            nc.sync.dma_start(out=br_sb[:], in_=br.rearrange("(c p) -> p c", p=P))

        def quantize(src, width, tag, cuts=()):
            codes = tile([P, width], U32, tag + "_codes")
            planes = tile([P, width], U8, tag + "_planes")
            for c0, c1 in zip((0, *cuts), (*cuts, width)):
                nc.vector.quantize_mx(
                    out=codes[:, c0:c1].bitcast(FP8X4), scales=planes[:, c0:c1], in_=src[:, PACK * c0 : PACK * c1]
                )
            return codes, planes

        def copy_on(engine, dst, src):
            if engine == "vector":
                nc.vector.tensor_copy(dst, src)
            else:
                nc.scalar.copy(dst, src)

        def quantize_w1(a, b, engines, cuts=()):
            grouped = tile([P, PACK, P, PACK], BF16, "w1_grouped%d" % a)
            width = P // len(engines)
            for u, engine in enumerate(engines):
                copy_on(
                    engine,
                    grouped[:, :, width * u : width * (u + 1), :].rearrange("p t m j -> p m t j"),
                    w1_raw[(a, b)][u][:].rearrange("p j (m t) -> p m t j", t=PACK),
                )
            return quantize(grouped[:].rearrange("p t m j -> p (t m j)"), PASS, "w1_%d_%d" % (a, b), cuts)

        def interleave(dst, src, engine="scalar"):
            copy_on(
                engine, dst.rearrange("p (c i) t -> p c t i", i=RUN), src.rearrange("p t (c i) -> p c t i", i=RUN)
            )

        def quantize_wp(b):
            grouped = tile([P, N, PACK], BF16, "wp_grouped", bufs=2)
            interleave(grouped[:], wp_raw[b][:])
            return quantize(grouped[:].rearrange("p n j -> p (n j)"), N, "wp_%d" % b)

        w1_q = {(0, 0): quantize_w1(0, 0, ("scalar",))}
        w1_q[(1, 0)] = quantize_w1(1, 0, ("scalar", "vector"), cuts=(P,))

        h_sb = {}

        def first_stage(s):
            b, t = divmod(s, PACK)
            banks = [bank("h_bank%d" % (2 * (s % 2) + n), [P, BANK]) for n in range(2)]
            for a in range(2):
                codes, planes = w1_q[(a, b)]
                for n in range(2):
                    cols = slice(BANK * n, BANK * (n + 1))
                    nc.tensor.matmul_mx(
                        out=banks[n][:],
                        lhsT=codes[:, P * t : P * (t + 1)].bitcast(FP8X4),
                        lhsT_scale=planes[:, P * t : P * (t + 1)],
                        rhs=v_words[a][:, cols].bitcast(FP8X4),
                        rhs_scale=v_planes[4 * a :, cols],
                        start=(a == 0),
                        stop=(a == 1),
                    )
            h_sb[s] = tile([P, S], F32, "h", bufs=6)
            for n in range(2):
                cols = slice(BANK * n, BANK * (n + 1))
                nc.vector.scalar_tensor_tensor(
                    out=h_sb[s][:, cols],
                    in0=banks[n][:],
                    scalar=vecs["gain"][:, b, t : t + 1],
                    in1=wear_sb[s][:, cols],
                    op0=ALU.mult,
                    op1=ALU.mult,
                )

        def posture_rows(s, xb_rows):
            b, t = divmod(s, PACK)
            picked = tile([P, PICK], F32, "picked_b", bufs=5)
            nc.vector.tensor_copy(picked[:], h_sb[s][:].indirect(pos2_sb[:]))
            size = tile([P, PICK], F32, "size_b", bufs=2)
            nc.scalar.activation(size[:], picked[:], ACT.Abs)
            nc.scalar.activation(xb_rows[:, t, :], size[:], ACT.Identity, bias=vecs["lift"][:, b, t : t + 1])

        def pick_rest(s):
            if s == PACK - 1:
                picked = tile([P, PICK], F32, "w1_grouped1")
            else:
                picked = tile([P, PICK], F32, "picked_a", bufs=2)
            nc.vector.tensor_copy(picked[:], h_sb[s][:].indirect(pos1_sb[:]))
            return picked

        def floor_rows(dst, picked, s):
            b, t = divmod(s, PACK)
            nc.vector.tensor_scalar(
                out=dst, in0=picked, scalar1=vecs["rest"][:, b, t : t + 1], scalar2=None, op0=ALU.max
            )

        def second_stage(banks, b, moving, stationary):
            codes, planes = moving
            for c in range(N // P):
                lhs, lhs_scale = stationary(b, c)
                nc.tensor.matmul_mx(
                    out=banks[c][:],
                    lhsT=lhs,
                    lhsT_scale=lhs_scale,
                    rhs=codes[:].bitcast(FP8X4),
                    rhs_scale=planes[:],
                    start=(b == 0),
                    stop=(b == 1),
                )

        wp_q = {}

        def wp_side(b, c):
            codes, planes = wp_q[b]
            return codes[:, P * c : P * (c + 1)].bitcast(FP8X4), planes[:, P * c : P * (c + 1)]

        def wr_side(b, c):
            return wr_sb[:, b, 2 * P * c : 2 * P * (c + 1)].bitcast(FP4X4), wr_planes[:, b, P * c : P * (c + 1)]

        xa_rows = tile([P, PACK, PICK], BF16, "xa_rows")
        xb_rows = tile([P, PACK, PICK], BF16, "xb_rows", bufs=2)
        first_stage(0)
        picked_a = {}
        for s in range(PACK):
            if s in (1, 2):
                w1_q[(s - 1, 1)] = quantize_w1(s - 1, 1, ("scalar",))
            first_stage(s + 1)
            posture_rows(s, xb_rows)
            if s > 0:
                floor_rows(xa_rows[:, s - 1, :], picked_a[s - 1][:], s - 1)
            picked_a[s] = pick_rest(s)
        wp_q[0] = quantize_wp(0)
        floor_rows(xa_rows[:, PACK - 1, :], picked_a[PACK - 1][:], PACK - 1)
        xb_grouped = tile([P, PICK, PACK], BF16, "xb_grouped")
        interleave(xb_grouped[:], xb_rows[:])
        xb_q = quantize(xb_grouped[:].rearrange("p n j -> p (n j)"), PICK, "xb0")
        xa_grouped = tile([P, PICK, PACK], BF16, "xa_grouped")
        interleave(xa_grouped[:], xa_rows[:])
        xa_q = quantize(xa_grouped[:].rearrange("p n j -> p (n j)"), PICK, "xa0")
        yb_banks = [bank("yb_bank%d" % c, [P, PICK]) for c in range(N // P)]
        second_stage(yb_banks, 0, xb_q, wp_side)

        xb_rows = tile([P, PACK, PICK], BF16, "xb_rows", bufs=2)
        for s in range(PACK, 2 * PACK):
            if s + 1 < 2 * PACK:
                first_stage(s + 1)
            posture_rows(s, xb_rows)
            if s == PACK:
                wp_q[1] = quantize_wp(1)
        ya_banks = [bank("h_bank%d" % c, [P, PICK]) for c in range(N // P)]
        second_stage(ya_banks, 0, xa_q, wr_side)

        xb_grouped = tile([P, PICK, PACK], BF16, "xb_grouped")
        interleave(xb_grouped[:], xb_rows[:])
        xb_q = quantize(xb_grouped[:].rearrange("p n j -> p (n j)"), PICK, "xb1")
        second_stage(yb_banks, 1, xb_q, wp_side)
        yb_sb = []
        for c in range(N // P):
            yb_sb.append(tile([P, PICK], F32, "wear%d" % c))
            nc.scalar.copy(yb_sb[c][:], yb_banks[c][:])

        picked = tile([P, PACK, PICK], F32, "wear7")
        xa_rows = tile([P, PACK, PICK], BF16, "xa_rows")
        for t in range(PACK):
            nc.vector.tensor_copy(picked[:, t, :], h_sb[PACK + t][:].indirect(pos1_sb[:]))
        for t in range(PACK):
            floor_rows(xa_rows[:, t, :], picked[:, t, :], PACK + t)
        xa_grouped = tile([P, PICK, PACK], BF16, "xb_grouped")
        interleave(xa_grouped[:], xa_rows[:], "vector")
        xa_q = quantize(xa_grouped[:].rearrange("p n j -> p (n j)"), PICK, "xa1")
        second_stage(ya_banks, 1, xa_q, wr_side)

        for c in range(N // P):
            result = tile([P, PICK], F32, "result", bufs=N // P)
            nc.vector.scalar_tensor_tensor(
                out=result[:],
                in0=ya_banks[c][:],
                scalar=br_sb[:, c : c + 1],
                in1=yb_sb[c][:],
                op0=ALU.add,
                op1=ALU.mult,
            )
            queue = nc.scalar if c % 2 == 0 else nc.sync
            queue.dma_start(out=out[P * c : P * (c + 1), :], in_=result[:])
